import numpy as np
import ml_dtypes


def mxq(x, axis, fmt="e4m3"):
    dtype, down = {"e4m3": (ml_dtypes.float8_e4m3fn, 7), "e5m2": (ml_dtypes.float8_e5m2, 14)}[fmt]
    v = np.moveaxis(np.asarray(x, np.float32).astype(ml_dtypes.bfloat16).astype(np.float64), axis, -1)
    blocks = v.reshape(v.shape[:-1] + (-1, 32))
    amax = np.abs(blocks).max(-1, keepdims=True)
    byte = np.maximum(np.where(amax > 0, np.frexp(amax)[1] - 1 + 127, 0) - down, 1)
    scale = np.exp2(byte - 127.0)
    codes = (blocks / scale).astype(np.float32).astype(dtype).astype(np.float64)
    return np.moveaxis((codes * scale).reshape(v.shape), -1, axis)


WIDE = False


def mx_kscale(k):
    if not WIDE:
        return np.ones(k)
    levels = np.array([10, -10, 5, -5, 0])
    if k % 512:
        return np.exp2(np.random.permutation(np.resize(levels, k // 32))).repeat(32)
    a = np.empty((k // 512, 16))
    for p in range(k // 512):
        a[p, :8] = np.random.permutation(np.resize(levels, 8))
        for g in range(8):
            far = levels[np.abs(levels - a[p, g]) >= 10]
            a[p, g + 8] = far[np.random.randint(len(far))]
    return np.exp2(a.ravel()).repeat(32)


BF16 = ml_dtypes.bfloat16


def bf(x):
    return np.asarray(x, np.float32).astype(BF16)


def f64(x):
    return np.asarray(x).astype(np.float64)


E2M1 = np.array([0.0, 0.5, 1.0, 1.5, 2.0, 3.0, 4.0, 6.0, -0.0, -0.5, -1.0, -1.5, -2.0, -3.0, -4.0, -6.0])


def pack_weight(w, fmt):
    k, n = w.shape
    w = f64(bf(w)).reshape(k // 32, 32, n)
    amax = np.abs(w).max(1)
    if fmt == "e4m3":
        byte = np.frexp(amax)[1] - 1 + 127 - 7
    else:
        mant, ex = np.frexp(amax / 6.0)
        byte = np.where(mant > 0.5, ex, ex - 1) + 127
    byte = np.clip(np.where(amax > 0, byte, 1), 1, 254)
    scaled = (w * np.exp2(127.0 - byte)[:, None, :]).reshape(k, n).astype(np.float32)
    by_word = np.ascontiguousarray(scaled.reshape(k // 512, 128, 4, n).transpose(0, 1, 3, 2))
    if fmt == "e4m3":
        words = by_word.astype(ml_dtypes.float8_e4m3fn).view(np.uint8)
    else:
        c = by_word.astype(ml_dtypes.float4_e2m1fn).view(np.uint8) & 0xF
        words = c[..., 0::2] | (c[..., 1::2] << 4)
    return np.ascontiguousarray(words), np.ascontiguousarray(byte.astype(np.uint8).reshape(k // 512, 16, n))


def unpack_weight(words, scales, fmt):
    g, p, n, _ = words.shape
    if fmt == "e4m3":
        vals = np.ascontiguousarray(words).view(ml_dtypes.float8_e4m3fn).astype(np.float64)
    else:
        nib = np.empty((g, p, n, 4), np.uint8)
        nib[..., 0::2] = words & 0xF
        nib[..., 1::2] = words >> 4
        vals = E2M1[nib]
    vals = vals * np.repeat(np.exp2(scales.astype(np.float64) - 127.0), 8, axis=1)[..., None]
    return vals.transpose(0, 1, 3, 2).reshape(g * 512, n)
def pack4(w):
    words, scales = pack_weight(w, "e2m1")
    return words.reshape(words.shape[0], 128, -1), scales


def unpack4(words, scales):
    return unpack_weight(words.reshape(words.shape[0], 128, -1, 2), scales, "e2m1")


M, K, F, V, D = 1024, 1024, 512, 2048, 1024


def setup_inputs():
    s = mx_kscale(K)
    u = mx_kscale(F)
    t = mx_kscale(V)
    hidden = bf(np.random.standard_normal((M, K)) * s)
    head = bf(np.random.standard_normal((K, V)) / np.sqrt(K) / s[:, None] * t)
    hashes = bf(np.random.standard_normal((M, F)) * u)
    bias = bf(0.3 * np.random.standard_normal(V) * t)
    green = np.random.standard_normal((F, V)) / np.sqrt(F) / u[:, None] * t
    green_words, green_scales = pack4(green)
    embed = np.random.standard_normal((V, D)) / np.sqrt(V) / t[:, None]
    embed_words, embed_scales = pack4(embed)
    return {"hidden": hidden, "head": head, "hashes": hashes, "bias": bias,
            "green_words": green_words, "green_scales": green_scales,
            "embed_words": embed_words, "embed_scales": embed_scales}


def reference(hidden, head, hashes, bias, green_words, green_scales, embed_words, embed_scales):
    logits = mxq(f64(hidden), 1, "e4m3") @ mxq(f64(head), 0, "e4m3")
    push = mxq(f64(hashes), 1, "e4m3") @ unpack4(green_words, green_scales)
    r = np.maximum(logits + push + f64(bias), 0.0)
    return mxq(r, 1, "e4m3") @ unpack4(embed_words, embed_scales)

@@ -1,0 +1,329 @@
+from contextlib import ExitStack
+
+import concourse.mybir as mybir
+from concourse.masks import make_identity
+
+M, K, F, V, D = 1024, 1024, 512, 2048, 1024
+FLOPS = 2 * M * (K * V + F * V + V * D)
+
+F32 = mybir.dt.float32
+BF16 = mybir.dt.bfloat16
+U32 = mybir.dt.uint32
+I32 = mybir.dt.int32
+U8 = mybir.dt.uint8
+FP8X4 = mybir.dt.float8_e4m3fn_x4
+FP4X4 = mybir.dt.float4_e2m1fn_x4
+ACT = mybir.ActivationFunctionType
+ALU = mybir.AluOpType
+
+P = 128
+PASS = 512
+HALF = 512
+GROUPS = V // PASS
+HASH = 2
+BANKS = 8
+
+
+def tile_watermarked_head_feedback_s3_kernel(
+    tc, hidden, head, hashes, bias, green_words, green_scales, embed_words, embed_scales, out
+):
+    nc = tc.nc
+    with ExitStack() as ctx:
+        sb = ctx.enter_context(tc.tile_pool(name="sb", bufs=1))
+        ps = ctx.enter_context(tc.psum_pool(name="ps", bufs=1))
+        ctx.enter_context(tc.manual_schedule())
+
+        def sbuf(name, shape, dtype, tag=""):
+            return sb.tile(shape, dtype, name=name, tag=tag or name, align_bytes=64)
+
+        def bank(i):
+            return ps.tile([P, 512], F32, name="bank%d" % i, tag="bank%d" % i)
+
+        pos_raw = {}
+        pos_wide = {}
+        pos_mx = {}
+        head_raw = {}
+        head_wide = {}
+        vocab_mx = {}
+        green_raw = {}
+        turned = {}
+        logit = {}
+        r_raw = {}
+        r_wide = {}
+        r_mx = {}
+
+        def load_positions(h, c):
+            raw = sbuf("pos_raw%d%d" % (h, c), [P, 4, PASS], BF16)
+            rows = slice(HALF * h, HALF * (h + 1))
+            src = hashes[rows, :] if c == HASH else hidden[rows, PASS * c : PASS * (c + 1)]
+            nc.sync.dma_start(out=raw[:], in_=src.rearrange("(p a) k -> p a k", a=4))
+            for b in range(2):
+                pos_raw[h, c, b] = raw[:].bitcast(F32)[:, 2 * b : 2 * b + 2, :]
+
+        def load_head(g, c):
+            raw = sbuf("head%d%d" % (g, c), [P, 4, PASS], BF16)
+            rows = head[PASS * c : PASS * (c + 1), PASS * g : PASS * (g + 1)]
+            nc.sync.dma_start(out=raw[:], in_=rows.rearrange("(p j) v -> p j v", j=4))
+            head_raw[g, c] = raw
+
+        def load_green(g):
+            raw = sbuf("green%d" % g, [P, 2 * PASS], U8)
+            src = green_words[0][:, 2 * PASS * g : 2 * PASS * (g + 1)]
+            nc.sync.dma_start(out=raw[:].bitcast(I32), in_=src.bitcast(I32))
+            green_raw[g] = raw
+
+        def turn(h, c, b, i):
+            words = pos_raw[h, c, b]
+            xt = bank(i)
+            for a in range(2):
+                for u in range(2):
+                    s = 2 * a + u
+                    nc.tensor.transpose(xt[:, P * s : P * (s + 1)], words[:, a, u:256:2], ident[:])
+            turned[h, c, b] = xt
+
+        def drain_turned(h, c, b, on_vector=False):
+            if b == 0:
+                pos_wide[h, c] = sbuf("pos_wide%d%d" % (h, c), [P, 4 * HALF], BF16, tag="pos_wide%d" % c)
+            dst = pos_wide[h, c][:].bitcast(F32)[:, 512 * b : 512 * (b + 1)]
+            dst = dst.rearrange("p (a r u) -> p a r u", a=2, u=2)
+            src = turned[h, c, b][:].rearrange("p (a u r) -> p a r u", a=2, u=2)
+            if on_vector:
+                nc.vector.tensor_copy(out=dst, in_=src)
+            else:
+                nc.scalar.copy(out=dst, in_=src)
+
+        def quantize(name, wide):
+            codes = sbuf(name + "_codes", [P, 512], U32)
+            scales = sbuf(name + "_scales", [P, 512], U8)
+            nc.vector.quantize_mx(out=codes[:].bitcast(FP8X4), scales=scales[:], in_=wide[:])
+            return codes, scales
+
+        def quantize_pos(h, c):
+            pos_mx[h, c] = quantize("pos%d%d" % (h, c), pos_wide[h, c])
+
+        def widen_head(g, c, on_scalar=False):
+            wide = sbuf("head_wide%d%d" % (g, c), [P, 4 * PASS], BF16, tag="head_wide%d" % c)
+            dst = wide[:].rearrange("p (t m e j) -> p m t e j", t=4, e=2, j=4)
+            src = head_raw[g, c][:].rearrange("p j (m e t) -> p m t e j", t=4, e=2)
+            if on_scalar:
+                nc.scalar.copy(out=dst, in_=src)
+            else:
+                nc.vector.tensor_copy(out=dst, in_=src)
+            head_wide[g, c] = wide
+
+        def quantize_head(g, c):
+            codes, scales = quantize("head%d%d" % (g, c), head_wide[g, c])
+            for t in range(4):
+                cols = slice(P * t, P * (t + 1))
+                vocab_mx[g, c, t] = (codes[:, cols].bitcast(FP8X4), scales[:, cols])
+
+        green_sorted = {}
+
+        def sort_green_codes(g):
+            codes = sbuf("green_codes%d" % g, [P, 2 * PASS], U8)
+            nc.vector.tensor_copy(
+                out=codes[:].rearrange("p (t m y) -> p t m y", t=4, y=2),
+                in_=green_raw[g][:].rearrange("p (m t y) -> p t m y", t=4, y=2),
+            )
+            green_sorted[g] = codes
+
+        def sort_green_scales(g):
+            scales = sbuf("green_scales%d" % g, [P, PASS], U8)
+            nc.vector.tensor_copy(
+                out=scales[:].rearrange("p (t m) -> p t m", t=4),
+                in_=green_plane[:, PASS * g : PASS * (g + 1)].rearrange("p (m t) -> p t m", t=4),
+            )
+            for t in range(4):
+                codes = green_sorted[g][:, 2 * P * t : 2 * P * (t + 1)]
+                vocab_mx[g, HASH, t] = (codes.bitcast(FP4X4), scales[:, P * t : P * (t + 1)])
+
+        def logit_pass(h, g, t, c, i):
+            if c == 0:
+                logit[h, g, t] = bank(i)
+            codes, scales = vocab_mx[g, c, t]
+            nc.tensor.matmul_mx(
+                out=logit[h, g, t][:],
+                lhsT=codes,
+                lhsT_scale=scales,
+                rhs=pos_mx[h, c][0][:].bitcast(FP8X4),
+                rhs_scale=pos_mx[h, c][1][:],
+                start=(c == 0),
+                stop=(c == HASH),
+            )
+
+        def rectify(h, g, t, on_vector=False):
+            if t == 0:
+                r_raw[h, g] = sbuf("r_raw%d%d" % (h, g), [P, 4, HALF], BF16)
+            column = bias_f32[:, 4 * g + t : 4 * g + t + 1]
+            if on_vector:
+                nc.vector.tensor_scalar(
+                    out=r_raw[h, g][:, t, :], in0=logit[h, g, t][:], scalar1=column, scalar2=0.0,
+                    op0=ALU.add, op1=ALU.max,
+                )
+            else:
+                nc.scalar.activation(out=r_raw[h, g][:, t, :], in_=logit[h, g, t][:], func=ACT.Relu, bias=column)
+
+        def widen_r(h, g, on_scalar=False):
+            wide = sbuf("r_wide%d%d" % (h, g), [P, 4 * HALF], BF16, tag="r_wide%d" % (len(r_wide) % 3))
+            dst = wide[:].rearrange("p (n i t) -> p n t i", i=4, t=4)
+            src = r_raw[h, g][:].rearrange("p t (n i) -> p n t i", i=4)
+            if on_scalar:
+                nc.scalar.copy(out=dst, in_=src)
+            else:
+                nc.vector.tensor_copy(out=dst, in_=src)
+            r_wide[h, g] = wide
+
+        def quantize_r(h, g):
+            r_mx[h, g] = quantize("r%d%d" % (h, g), r_wide[h, g])
+
+        def mix(h, tile, d, i):
+            acc = bank(i)
+            cols = slice(P * tile, P * (tile + 1))
+            for g in range(GROUPS):
+                codes, scales = r_mx[h, g]
+                nc.tensor.matmul_mx(
+                    out=acc[:],
+                    lhsT=codes[:, cols].bitcast(FP8X4),
+                    lhsT_scale=scales[:, cols],
+                    rhs=embed_codes[g][:, 1024 * d : 1024 * (d + 1)].bitcast(FP4X4),
+                    rhs_scale=embed_plane[:, g, 512 * d : 512 * (d + 1)],
+                    start=(g == 0),
+                    stop=(g == GROUPS - 1),
+                )
+            return acc
+
+        def store(h, tile, d, acc, on_vector):
+            n = 8 * h + 2 * tile + d
+            res = sbuf("res%d" % n, [P, 512], F32, tag="res%d" % (n % 6))
+            if on_vector:
+                nc.vector.tensor_copy(out=res[:], in_=acc[:])
+            else:
+                nc.scalar.copy(out=res[:], in_=acc[:])
+            rows = out[HALF * h : HALF * (h + 1), 512 * d : 512 * (d + 1)]
+            nc.sync.dma_start(out=rows.rearrange("(p a) d -> p a d", a=4)[:, tile, :], in_=res[:])
+
+        ident = sbuf("ident", [P, P], F32)
+        make_identity(nc, ident[:])
+        green_plane = sbuf("green_plane", [P, V], U8)
+        embed_plane = sbuf("embed_plane", [P, GROUPS, D], U8)
+        nc.vector.memset(green_plane[:].bitcast(I32), 0)
+        nc.vector.memset(embed_plane[:].bitcast(I32), 0)
+        bias_raw = sbuf("bias_raw", [P, GROUPS, 4], BF16)
+        bias_f32 = sbuf("bias_f32", [P, 4 * GROUPS], F32)
+        nc.scalar.dma_start(out=bias_raw[:], in_=bias.rearrange("(g p t) -> p g t", g=GROUPS, t=4))
+        for q in range(4):
+            nc.gpsimd.dma_start(
+                out=green_plane[32 * q : 32 * q + 4, :].bitcast(I32),
+                in_=green_scales[0][4 * q : 4 * q + 4, :].bitcast(I32),
+            )
+
+        load_positions(0, 0)
+        load_green(0)
+        load_head(0, 0)
+        load_positions(0, 1)
+        load_head(0, 1)
+        load_positions(0, HASH)
+        load_head(1, 0)
+        load_green(1)
+        load_head(1, 1)
+        for c in range(3):
+            load_positions(1, c)
+        for g in range(2, GROUPS):
+            load_head(g, 0)
+            load_green(g)
+            load_head(g, 1)
+        embed_codes = []
+        for g in range(GROUPS):
+            words = sbuf("embed%d" % g, [P, 2 * D], U8)
+            nc.sync.dma_start(out=words[:].bitcast(I32), in_=embed_words[g].bitcast(I32))
+            embed_codes.append(words)
+        for q in range(4):
+            nc.sync.dma_start(
+                out=embed_plane[32 * q : 32 * q + 4, :, :].bitcast(I32),
+                in_=embed_scales[:, 4 * q : 4 * q + 4, :].rearrange("g r n -> r g n").bitcast(I32),
+            )
+
+        nc.scalar.activation(out=bias_f32[:], in_=bias_raw[:].rearrange("p g t -> p (g t)"), func=ACT.Identity)
+
+        def turn_pass(h, c, first_bank):
+            for b in range(2):
+                turn(h, c, b, first_bank + b)
+                drain_turned(h, c, b)
+
+        def logit_passes(h, g, c):
+            for t in range(4):
+                logit_pass(h, g, t, c, 4 + t)
+
+        def prepare_group(g):
+            widen_head(g, 0)
+            sort_green_codes(g)
+            quantize_head(g, 0)
+            widen_head(g, 1)
+            sort_green_scales(g)
+            quantize_head(g, 1)
+
+        def logit_tile(h, g, t, i):
+            for c in range(3):
+                logit_pass(h, g, t, c, i)
+            rectify(h, g, t)
+
+        sort_green_codes(0)
+        turn_pass(0, 0, 0)
+        turn_pass(0, 1, 2)
+        widen_head(0, 0)
+        quantize_head(0, 0)
+        quantize_pos(0, 0)
+        logit_passes(0, 0, 0)
+        turn_pass(0, HASH, 0)
+        widen_head(0, 1)
+        quantize_pos(0, 1)
+        quantize_head(0, 1)
+        sort_green_scales(0)
+        widen_head(1, 0)
+        quantize_pos(0, HASH)
+        logit_passes(0, 0, 1)
+        logit_passes(0, 0, HASH)
+        for t in range(4):
+            rectify(0, 0, t)
+        quantize_head(1, 0)
+        widen_head(1, 1)
+        sort_green_codes(1)
+        quantize_head(1, 1)
+        sort_green_scales(1)
+        turn_pass(1, 0, 2)
+        logit_tile(0, 1, 0, 4)
+        logit_tile(0, 1, 1, 5)
+        turn_pass(1, 1, 0)
+        logit_tile(0, 1, 2, 6)
+        turn_pass(1, HASH, 2)
+        logit_tile(0, 1, 3, 7)
+        quantize_pos(1, 0)
+        widen_head(2, 0)
+        quantize_pos(1, 1)
+        sort_green_codes(2)
+        quantize_pos(1, HASH)
+        quantize_head(2, 0)
+        widen_head(2, 1)
+        sort_green_scales(2)
+        quantize_head(2, 1)
+        prepare_group(3)
+        for c in range(3):
+            logit_passes(1, 0, c)
+        for t in range(4):
+            rectify(1, 0, t)
+        steps = [(1, 1), (0, 2), (0, 3), (1, 2), (1, 3)]
+        for n, (h, g) in enumerate(steps):
+            for t in range(4):
+                logit_tile(h, g, t, 4 * (n % 2) + t)
+        order = [(h, g) for h in range(2) for g in range(GROUPS)]
+        widen_r(*order[0])
+        for n in range(1, len(order)):
+            widen_r(*order[n])
+            quantize_r(*order[n - 1])
+        quantize_r(*order[-1])
+
+        for h in range(2):
+            for tile in range(4):
+                for d in range(2):
+                    acc = mix(h, tile, d, (4 + 2 * tile + d) % BANKS)
+                    store(h, tile, d, acc, on_vector=(h == 1 and d == 1))

@@ -40,6 +40,8 @@ def tile_watermarked_head_feedback_s3_kernel(
             return ps.tile([P, 512], F32, name="bank%d" % i, tag="bank%d" % i)
 
         pos_raw = {}
+        pos_tile = {}
+        pos_sorted = {}
         pos_wide = {}
         pos_mx = {}
         head_raw = {}
@@ -57,6 +59,7 @@ def tile_watermarked_head_feedback_s3_kernel(
             rows = slice(HALF * h, HALF * (h + 1))
             src = hashes[rows, :] if c == HASH else hidden[rows, PASS * c : PASS * (c + 1)]
             nc.sync.dma_start(out=raw[:], in_=src.rearrange("(p a) k -> p a k", a=4))
+            pos_tile[h, c] = raw
             for b in range(2):
                 pos_raw[h, c, b] = raw[:].bitcast(F32)[:, 2 * b : 2 * b + 2, :]
 
@@ -67,10 +70,20 @@ def tile_watermarked_head_feedback_s3_kernel(
             head_raw[g, c] = raw
 
         def load_green(g):
-            raw = sbuf("green%d" % g, [P, 2 * PASS], U8)
-            src = green_words[0][:, 2 * PASS * g : 2 * PASS * (g + 1)]
+            raw = sbuf("green%d" % g, [P, 4 * PASS], U8)
+            src = green_words[0][:, 2 * PASS * g : 2 * PASS * (g + 2)]
             nc.sync.dma_start(out=raw[:].bitcast(I32), in_=src.bitcast(I32))
-            green_raw[g] = raw
+            green_raw[g] = raw[:, : 2 * PASS]
+            green_raw[g + 1] = raw[:, 2 * PASS :]
+
+        def sort_words(h, c, on_vector=False):
+            words = sbuf("pos_sorted%d%d" % (h, c), [P, 4, 2, P], F32, tag="pos_sorted%d" % (c % 2))
+            src = pos_tile[h, c][:].bitcast(F32).rearrange("p a (r u) -> p a u r", u=2)
+            if on_vector:
+                nc.vector.tensor_copy(out=words[:], in_=src)
+            else:
+                nc.scalar.copy(out=words[:], in_=src)
+            pos_sorted[h, c] = words
 
         def turn(h, c, b, i):
             words = pos_raw[h, c, b]
@@ -78,7 +91,11 @@ def tile_watermarked_head_feedback_s3_kernel(
             for a in range(2):
                 for u in range(2):
                     s = 2 * a + u
-                    nc.tensor.transpose(xt[:, P * s : P * (s + 1)], words[:, a, u:256:2], ident[:])
+                    if (h, c) in pos_sorted:
+                        src = pos_sorted[h, c][:, 2 * b + a, u, :]
+                    else:
+                        src = words[:, a, u:256:2]
+                    nc.tensor.transpose(xt[:, P * s : P * (s + 1)], src, ident[:])
             turned[h, c, b] = xt
 
         def drain_turned(h, c, b, on_vector=False):
@@ -101,14 +118,13 @@ def tile_watermarked_head_feedback_s3_kernel(
         def quantize_pos(h, c):
             pos_mx[h, c] = quantize("pos%d%d" % (h, c), pos_wide[h, c])
 
-        def widen_head(g, c, on_scalar=False):
+        def widen_head(g, c, scalar_share=0):
             wide = sbuf("head_wide%d%d" % (g, c), [P, 4 * PASS], BF16, tag="head_wide%d" % c)
             dst = wide[:].rearrange("p (t m e j) -> p m t e j", t=4, e=2, j=4)
             src = head_raw[g, c][:].rearrange("p j (m e t) -> p m t e j", t=4, e=2)
-            if on_scalar:
-                nc.scalar.copy(out=dst, in_=src)
-            else:
-                nc.vector.tensor_copy(out=dst, in_=src)
+            if scalar_share:
+                nc.scalar.copy(out=dst[:, :scalar_share], in_=src[:, :scalar_share])
+            nc.vector.tensor_copy(out=dst[:, scalar_share:], in_=src[:, scalar_share:])
             head_wide[g, c] = wide
 
         def quantize_head(g, c):
@@ -123,7 +139,7 @@ def tile_watermarked_head_feedback_s3_kernel(
             codes = sbuf("green_codes%d" % g, [P, 2 * PASS], U8)
             nc.vector.tensor_copy(
                 out=codes[:].rearrange("p (t m y) -> p t m y", t=4, y=2),
-                in_=green_raw[g][:].rearrange("p (m t y) -> p t m y", t=4, y=2),
+                in_=green_raw[g].rearrange("p (m t y) -> p t m y", t=4, y=2),
             )
             green_sorted[g] = codes
 
@@ -137,8 +153,8 @@ def tile_watermarked_head_feedback_s3_kernel(
                 codes = green_sorted[g][:, 2 * P * t : 2 * P * (t + 1)]
                 vocab_mx[g, HASH, t] = (codes.bitcast(FP4X4), scales[:, P * t : P * (t + 1)])
 
-        def logit_pass(h, g, t, c, i):
-            if c == 0:
+        def logit_pass(h, g, t, c, i, first=0, last=HASH):
+            if c == first:
                 logit[h, g, t] = bank(i)
             codes, scales = vocab_mx[g, c, t]
             nc.tensor.matmul_mx(
@@ -147,14 +163,14 @@ def tile_watermarked_head_feedback_s3_kernel(
                 lhsT_scale=scales,
                 rhs=pos_mx[h, c][0][:].bitcast(FP8X4),
                 rhs_scale=pos_mx[h, c][1][:],
-                start=(c == 0),
-                stop=(c == HASH),
+                start=(c == first),
+                stop=(c == last),
             )
 
         def rectify(h, g, t, on_vector=False):
             if t == 0:
                 r_raw[h, g] = sbuf("r_raw%d%d" % (h, g), [P, 4, HALF], BF16)
-            column = bias_f32[:, 4 * g + t : 4 * g + t + 1]
+            column = bias_raw[:, g, t : t + 1]
             if on_vector:
                 nc.vector.tensor_scalar(
                     out=r_raw[h, g][:, t, :], in0=logit[h, g, t][:], scalar1=column, scalar2=0.0,
@@ -176,62 +192,86 @@ def tile_watermarked_head_feedback_s3_kernel(
         def quantize_r(h, g):
             r_mx[h, g] = quantize("r%d%d" % (h, g), r_wide[h, g])
 
-        def mix(h, tile, d, i):
-            acc = bank(i)
-            cols = slice(P * tile, P * (tile + 1))
-            for g in range(GROUPS):
-                codes, scales = r_mx[h, g]
-                nc.tensor.matmul_mx(
-                    out=acc[:],
-                    lhsT=codes[:, cols].bitcast(FP8X4),
-                    lhsT_scale=scales[:, cols],
-                    rhs=embed_codes[g][:, 1024 * d : 1024 * (d + 1)].bitcast(FP4X4),
-                    rhs_scale=embed_plane[:, g, 512 * d : 512 * (d + 1)],
-                    start=(g == 0),
-                    stop=(g == GROUPS - 1),
-                )
-            return acc
+        def mix_pass(acc, h, tile, g, first, width):
+            codes, scales = r_mx[h, g]
+            rows = slice(P * tile, P * (tile + 1))
+            nc.tensor.matmul_mx(
+                out=acc[:, :width],
+                lhsT=codes[:, rows].bitcast(FP8X4),
+                lhsT_scale=scales[:, rows],
+                rhs=embed_codes[g][:, 2 * first : 2 * (first + width)].bitcast(FP4X4),
+                rhs_scale=embed_plane[:, g, first : first + width],
+                start=(g == 0),
+                stop=(g == GROUPS - 1),
+            )
 
-        def store(h, tile, d, acc, on_vector):
-            n = 8 * h + 2 * tile + d
-            res = sbuf("res%d" % n, [P, 512], F32, tag="res%d" % (n % 6))
+        stored = []
+
+        def store(acc, h, tile, first, width, on_vector):
+            n = len(stored)
+            stored.append(n)
+            res = sbuf("res%d" % n, [P, width], F32, tag="res%d" % (n % 6))
             if on_vector:
-                nc.vector.tensor_copy(out=res[:], in_=acc[:])
+                nc.vector.tensor_copy(out=res[:], in_=acc[:, :width])
             else:
-                nc.scalar.copy(out=res[:], in_=acc[:])
-            rows = out[HALF * h : HALF * (h + 1), 512 * d : 512 * (d + 1)]
+                nc.scalar.copy(out=res[:], in_=acc[:, :width])
+            rows = out[HALF * h : HALF * (h + 1), first : first + width]
             nc.sync.dma_start(out=rows.rearrange("(p a) d -> p a d", a=4)[:, tile, :], in_=res[:])
 
+        ones = sbuf("ones", [P, 4 * P], BF16)
+        ones_codes = sbuf("ones_codes", [P, P], U32)
+        ones_scales = sbuf("ones_scales", [P, P], U8)
+        nc.vector.memset(ones[:], 1.0)
+        nc.vector.quantize_mx(out=ones_codes[:].bitcast(FP8X4), scales=ones_scales[:], in_=ones[:])
+
+        def warm(passes):
+            idle = bank(7)
+            for n in range(passes):
+                nc.tensor.matmul_mx(
+                    out=idle[:, :P],
+                    lhsT=ones_codes[:].bitcast(FP8X4),
+                    lhsT_scale=ones_scales[:],
+                    rhs=ones_codes[:].bitcast(FP8X4),
+                    rhs_scale=ones_scales[:],
+                    start=True,
+                    stop=True,
+                )
+
+        ident_bf16 = sbuf("ident_bf16", [P, P], BF16)
         ident = sbuf("ident", [P, P], F32)
-        make_identity(nc, ident[:])
+        make_identity(nc, ident_bf16[:])
+        nc.scalar.activation(out=ident[:], in_=ident_bf16[:], func=ACT.Identity)
         green_plane = sbuf("green_plane", [P, V], U8)
         embed_plane = sbuf("embed_plane", [P, GROUPS, D], U8)
         nc.vector.memset(green_plane[:].bitcast(I32), 0)
         nc.vector.memset(embed_plane[:].bitcast(I32), 0)
         bias_raw = sbuf("bias_raw", [P, GROUPS, 4], BF16)
-        bias_f32 = sbuf("bias_f32", [P, 4 * GROUPS], F32)
-        nc.scalar.dma_start(out=bias_raw[:], in_=bias.rearrange("(g p t) -> p g t", g=GROUPS, t=4))
-        for q in range(4):
-            nc.gpsimd.dma_start(
-                out=green_plane[32 * q : 32 * q + 4, :].bitcast(I32),
-                in_=green_scales[0][4 * q : 4 * q + 4, :].bitcast(I32),
-            )
+
+        def load_green_scales():
+            for q in range(4):
+                nc.sync.dma_start(
+                    out=green_plane[32 * q : 32 * q + 4, :].bitcast(I32),
+                    in_=green_scales[0][4 * q : 4 * q + 4, :].bitcast(I32),
+                )
 
         load_positions(0, 0)
-        load_green(0)
         load_head(0, 0)
         load_positions(0, 1)
         load_head(0, 1)
         load_positions(0, HASH)
+        load_green(0)
+        load_green_scales()
+        load_positions(1, 0)
+        nc.sync.dma_start(out=bias_raw[:], in_=bias.rearrange("(g p t) -> p g t", g=GROUPS, t=4))
+        load_positions(1, 1)
+        load_positions(1, HASH)
         load_head(1, 0)
-        load_green(1)
         load_head(1, 1)
-        for c in range(3):
-            load_positions(1, c)
-        for g in range(2, GROUPS):
-            load_head(g, 0)
-            load_green(g)
-            load_head(g, 1)
+        load_head(2, 0)
+        load_green(2)
+        load_head(2, 1)
+        load_head(3, 0)
+        load_head(3, 1)
         embed_codes = []
         for g in range(GROUPS):
             words = sbuf("embed%d" % g, [P, 2 * D], U8)
@@ -243,7 +283,6 @@ def tile_watermarked_head_feedback_s3_kernel(
                 in_=embed_scales[:, 4 * q : 4 * q + 4, :].rearrange("g r n -> r g n").bitcast(I32),
             )
 
-        nc.scalar.activation(out=bias_f32[:], in_=bias_raw[:].rearrange("p g t -> p (g t)"), func=ACT.Identity)
 
         def turn_pass(h, c, first_bank):
             for b in range(2):
@@ -267,63 +306,84 @@ def tile_watermarked_head_feedback_s3_kernel(
                 logit_pass(h, g, t, c, i)
             rectify(h, g, t)
 
-        sort_green_codes(0)
+        warm(14)
         turn_pass(0, 0, 0)
-        turn_pass(0, 1, 2)
+        warm(8)
         widen_head(0, 0)
-        quantize_head(0, 0)
         quantize_pos(0, 0)
-        logit_passes(0, 0, 0)
-        turn_pass(0, HASH, 0)
+        quantize_head(0, 0)
+        turn_pass(0, 1, 2)
         widen_head(0, 1)
         quantize_pos(0, 1)
         quantize_head(0, 1)
-        sort_green_scales(0)
-        widen_head(1, 0)
-        quantize_pos(0, HASH)
-        logit_passes(0, 0, 1)
-        logit_passes(0, 0, HASH)
         for t in range(4):
-            rectify(0, 0, t)
-        quantize_head(1, 0)
-        widen_head(1, 1)
+            logit_pass(0, 0, t, 0, 4 + t)
+        turn_pass(0, HASH, 0)
+        sort_green_codes(0)
+        sort_green_scales(0)
+        quantize_pos(0, HASH)
         sort_green_codes(1)
-        quantize_head(1, 1)
         sort_green_scales(1)
+        for t in range(4):
+            logit_pass(0, 0, t, 1, 4 + t)
         turn_pass(1, 0, 2)
-        logit_tile(0, 1, 0, 4)
-        logit_tile(0, 1, 1, 5)
-        turn_pass(1, 1, 0)
-        logit_tile(0, 1, 2, 6)
-        turn_pass(1, HASH, 2)
-        logit_tile(0, 1, 3, 7)
+        sort_words(1, 1, True)
+        for t in range(4):
+            logit_pass(0, 0, t, HASH, 4 + t)
+        rectify(0, 0, 0)
+        rectify(0, 0, 1)
+        sort_words(1, HASH, True)
         quantize_pos(1, 0)
-        widen_head(2, 0)
+        turn_pass(1, 1, 0)
+        turn_pass(1, HASH, 2)
+        rectify(0, 0, 2)
+        rectify(0, 0, 3)
+        widen_head(1, 0)
         quantize_pos(1, 1)
-        sort_green_codes(2)
+        quantize_head(1, 0)
         quantize_pos(1, HASH)
+        widen_head(1, 1)
+        ring = [4, 5, 0, 1, 2, 3, 6, 7]
+        for c in range(3):
+            for t in range(4):
+                logit_pass(1, 0, t, c, ring[t])
+        for t in range(4):
+            rectify(1, 0, t)
+        widen_head(2, 0)
+        quantize_head(1, 1)
+        sort_green_codes(2)
         quantize_head(2, 0)
         widen_head(2, 1)
         sort_green_scales(2)
         quantize_head(2, 1)
         prepare_group(3)
-        for c in range(3):
-            logit_passes(1, 0, c)
+        for c in (0, HASH, 1):
+            for t in range(4):
+                logit_pass(0, 1, t, c, ring[4 + t], last=1)
         for t in range(4):
-            rectify(1, 0, t)
-        steps = [(1, 1), (0, 2), (0, 3), (1, 2), (1, 3)]
+            rectify(0, 1, t)
+        steps = [(1, 1), (0, 2), (1, 2), (0, 3), (1, 3)]
         for n, (h, g) in enumerate(steps):
             for t in range(4):
-                logit_tile(h, g, t, 4 * (n % 2) + t)
-        order = [(h, g) for h in range(2) for g in range(GROUPS)]
+                logit_tile(h, g, t, ring[(4 * n + t) % 8])
+        order = [(0, 0), (0, 1), (0, 2), (1, 0), (0, 3), (1, 1), (1, 2), (1, 3)]
         widen_r(*order[0])
         for n in range(1, len(order)):
             widen_r(*order[n])
             quantize_r(*order[n - 1])
         quantize_r(*order[-1])
 
-        for h in range(2):
-            for tile in range(4):
-                for d in range(2):
-                    acc = mix(h, tile, d, (4 + 2 * tile + d) % BANKS)
-                    store(h, tile, d, acc, on_vector=(h == 1 and d == 1))
+        blocks = [(h, tile, 512 * d, 512) for h in range(2) for tile in range(4) for d in range(2)]
+        blocks = blocks[:-1] + [(1, 3, 512 + P * j, P) for j in range(4)]
+        accs = [bank(ring[4 + n]) for n in range(4)]
+        for g in range(GROUPS):
+            for acc, (h, tile, first, width) in zip(accs, blocks):
+                mix_pass(acc, h, tile, g, first, width)
+        for acc, block in zip(accs, blocks):
+            store(acc, *block, on_vector=False)
+        for n in range(4, len(blocks)):
+            h, tile, first, width = blocks[n]
+            acc = bank(ring[(4 + n) % BANKS])
+            for g in range(GROUPS):
+                mix_pass(acc, h, tile, g, first, width)
+            store(acc, h, tile, first, width, on_vector=(n >= 8 and n % 2 == 1))

from contextlib import ExitStack

import concourse.mybir as mybir
from concourse.masks import make_identity

M, K, F, V, D = 1024, 1024, 512, 2048, 1024
FLOPS = 2 * M * (K * V + F * V + V * D)

F32 = mybir.dt.float32
BF16 = mybir.dt.bfloat16
U32 = mybir.dt.uint32
I32 = mybir.dt.int32
U8 = mybir.dt.uint8
FP8X4 = mybir.dt.float8_e4m3fn_x4
FP4X4 = mybir.dt.float4_e2m1fn_x4
ACT = mybir.ActivationFunctionType
ALU = mybir.AluOpType

P = 128
PASS = 512
HALF = 512
GROUPS = V // PASS
HASH = 2
BANKS = 8


def tile_watermarked_head_feedback_s3_kernel(
    tc, hidden, head, hashes, bias, green_words, green_scales, embed_words, embed_scales, out
):
    nc = tc.nc
    with ExitStack() as ctx:
        sb = ctx.enter_context(tc.tile_pool(name="sb", bufs=1))
        ps = ctx.enter_context(tc.psum_pool(name="ps", bufs=1))
        ctx.enter_context(tc.manual_schedule())

        def sbuf(name, shape, dtype, tag=""):
            return sb.tile(shape, dtype, name=name, tag=tag or name, align_bytes=64)

        def bank(i):
            return ps.tile([P, 512], F32, name="bank%d" % i, tag="bank%d" % i)

        pos_raw = {}
        pos_tile = {}
        pos_sorted = {}
        pos_wide = {}
        pos_mx = {}
        head_raw = {}
        head_wide = {}
        vocab_mx = {}
        green_raw = {}
        turned = {}
        logit = {}
        r_raw = {}
        r_wide = {}
        r_mx = {}

        def load_positions(h, c):
            raw = sbuf("pos_raw%d%d" % (h, c), [P, 4, PASS], BF16)
            rows = slice(HALF * h, HALF * (h + 1))
            src = hashes[rows, :] if c == HASH else hidden[rows, PASS * c : PASS * (c + 1)]
            nc.sync.dma_start(out=raw[:], in_=src.rearrange("(p a) k -> p a k", a=4))
            pos_tile[h, c] = raw
            for b in range(2):
                pos_raw[h, c, b] = raw[:].bitcast(F32)[:, 2 * b : 2 * b + 2, :]

        def load_head(g, c):
            raw = sbuf("head%d%d" % (g, c), [P, 4, PASS], BF16)
            rows = head[PASS * c : PASS * (c + 1), PASS * g : PASS * (g + 1)]
            nc.sync.dma_start(out=raw[:], in_=rows.rearrange("(p j) v -> p j v", j=4))
            head_raw[g, c] = raw

        def load_green(g):
            raw = sbuf("green%d" % g, [P, 4 * PASS], U8)
            src = green_words[0][:, 2 * PASS * g : 2 * PASS * (g + 2)]
            nc.sync.dma_start(out=raw[:].bitcast(I32), in_=src.bitcast(I32))
            green_raw[g] = raw[:, : 2 * PASS]
            green_raw[g + 1] = raw[:, 2 * PASS :]

        def sort_words(h, c, on_vector=False):
            words = sbuf("pos_sorted%d%d" % (h, c), [P, 4, 2, P], F32, tag="pos_sorted%d" % (c % 2))
            src = pos_tile[h, c][:].bitcast(F32).rearrange("p a (r u) -> p a u r", u=2)
            if on_vector:
                nc.vector.tensor_copy(out=words[:], in_=src)
            else:
                nc.scalar.copy(out=words[:], in_=src)
            pos_sorted[h, c] = words

        def turn(h, c, b, i):
            words = pos_raw[h, c, b]
            xt = bank(i)
            for a in range(2):
                for u in range(2):
                    s = 2 * a + u
                    if (h, c) in pos_sorted:
                        src = pos_sorted[h, c][:, 2 * b + a, u, :]
                    else:
                        src = words[:, a, u:256:2]
                    nc.tensor.transpose(xt[:, P * s : P * (s + 1)], src, ident[:])
            turned[h, c, b] = xt

        def drain_turned(h, c, b, on_vector=False):
            if b == 0:
                pos_wide[h, c] = sbuf("pos_wide%d%d" % (h, c), [P, 4 * HALF], BF16, tag="pos_wide%d" % c)
            dst = pos_wide[h, c][:].bitcast(F32)[:, 512 * b : 512 * (b + 1)]
            dst = dst.rearrange("p (a r u) -> p a r u", a=2, u=2)
            src = turned[h, c, b][:].rearrange("p (a u r) -> p a r u", a=2, u=2)
            if on_vector:
                nc.vector.tensor_copy(out=dst, in_=src)
            else:
                nc.scalar.copy(out=dst, in_=src)

        def quantize(name, wide):
            codes = sbuf(name + "_codes", [P, 512], U32)
            scales = sbuf(name + "_scales", [P, 512], U8)
            nc.vector.quantize_mx(out=codes[:].bitcast(FP8X4), scales=scales[:], in_=wide[:])
            return codes, scales

        def quantize_pos(h, c):
            pos_mx[h, c] = quantize("pos%d%d" % (h, c), pos_wide[h, c])

        def widen_head(g, c, scalar_share=0):
            wide = sbuf("head_wide%d%d" % (g, c), [P, 4 * PASS], BF16, tag="head_wide%d" % c)
            dst = wide[:].rearrange("p (t m e j) -> p m t e j", t=4, e=2, j=4)
            src = head_raw[g, c][:].rearrange("p j (m e t) -> p m t e j", t=4, e=2)
            if scalar_share:
                nc.scalar.copy(out=dst[:, :scalar_share], in_=src[:, :scalar_share])
            nc.vector.tensor_copy(out=dst[:, scalar_share:], in_=src[:, scalar_share:])
            head_wide[g, c] = wide

        def quantize_head(g, c):
            codes, scales = quantize("head%d%d" % (g, c), head_wide[g, c])
            for t in range(4):
                cols = slice(P * t, P * (t + 1))
                vocab_mx[g, c, t] = (codes[:, cols].bitcast(FP8X4), scales[:, cols])

        green_sorted = {}

        def sort_green_codes(g):
            codes = sbuf("green_codes%d" % g, [P, 2 * PASS], U8)
            nc.vector.tensor_copy(
                out=codes[:].rearrange("p (t m y) -> p t m y", t=4, y=2),
                in_=green_raw[g].rearrange("p (m t y) -> p t m y", t=4, y=2),
            )
            green_sorted[g] = codes

        def sort_green_scales(g):
            scales = sbuf("green_scales%d" % g, [P, PASS], U8)
            nc.vector.tensor_copy(
                out=scales[:].rearrange("p (t m) -> p t m", t=4),
                in_=green_plane[:, PASS * g : PASS * (g + 1)].rearrange("p (m t) -> p t m", t=4),
            )
            for t in range(4):
                codes = green_sorted[g][:, 2 * P * t : 2 * P * (t + 1)]
                vocab_mx[g, HASH, t] = (codes.bitcast(FP4X4), scales[:, P * t : P * (t + 1)])

        def logit_pass(h, g, t, c, i, first=0, last=HASH):
            if c == first:
                logit[h, g, t] = bank(i)
            codes, scales = vocab_mx[g, c, t]
            nc.tensor.matmul_mx(
                out=logit[h, g, t][:],
                lhsT=codes,
                lhsT_scale=scales,
                rhs=pos_mx[h, c][0][:].bitcast(FP8X4),
                rhs_scale=pos_mx[h, c][1][:],
                start=(c == first),
                stop=(c == last),
            )

        def rectify(h, g, t, on_vector=False):
            if t == 0:
                r_raw[h, g] = sbuf("r_raw%d%d" % (h, g), [P, 4, HALF], BF16)
            column = bias_raw[:, g, t : t + 1]
            if on_vector:
                nc.vector.tensor_scalar(
                    out=r_raw[h, g][:, t, :], in0=logit[h, g, t][:], scalar1=column, scalar2=0.0,
                    op0=ALU.add, op1=ALU.max,
                )
            else:
                nc.scalar.activation(out=r_raw[h, g][:, t, :], in_=logit[h, g, t][:], func=ACT.Relu, bias=column)

        def widen_r(h, g, on_scalar=False):
            wide = sbuf("r_wide%d%d" % (h, g), [P, 4 * HALF], BF16, tag="r_wide%d" % (len(r_wide) % 3))
            dst = wide[:].rearrange("p (n i t) -> p n t i", i=4, t=4)
            src = r_raw[h, g][:].rearrange("p t (n i) -> p n t i", i=4)
            if on_scalar:
                nc.scalar.copy(out=dst, in_=src)
            else:
                nc.vector.tensor_copy(out=dst, in_=src)
            r_wide[h, g] = wide

        def quantize_r(h, g):
            r_mx[h, g] = quantize("r%d%d" % (h, g), r_wide[h, g])

        def mix_pass(acc, h, tile, g, first, width):
            codes, scales = r_mx[h, g]
            rows = slice(P * tile, P * (tile + 1))
            nc.tensor.matmul_mx(
                out=acc[:, :width],
                lhsT=codes[:, rows].bitcast(FP8X4),
                lhsT_scale=scales[:, rows],
                rhs=embed_codes[g][:, 2 * first : 2 * (first + width)].bitcast(FP4X4),
                rhs_scale=embed_plane[:, g, first : first + width],
                start=(g == 0),
                stop=(g == GROUPS - 1),
            )

        stored = []

        def store(acc, h, tile, first, width, on_vector):
            n = len(stored)
            stored.append(n)
            res = sbuf("res%d" % n, [P, width], F32, tag="res%d" % (n % 6))
            if on_vector:
                nc.vector.tensor_copy(out=res[:], in_=acc[:, :width])
            else:
                nc.scalar.copy(out=res[:], in_=acc[:, :width])
            rows = out[HALF * h : HALF * (h + 1), first : first + width]
            nc.sync.dma_start(out=rows.rearrange("(p a) d -> p a d", a=4)[:, tile, :], in_=res[:])

        ones = sbuf("ones", [P, 4 * P], BF16)
        ones_codes = sbuf("ones_codes", [P, P], U32)
        ones_scales = sbuf("ones_scales", [P, P], U8)
        nc.vector.memset(ones[:], 1.0)
        nc.vector.quantize_mx(out=ones_codes[:].bitcast(FP8X4), scales=ones_scales[:], in_=ones[:])

        def warm(passes):
            idle = bank(7)
            for n in range(passes):
                nc.tensor.matmul_mx(
                    out=idle[:, :P],
                    lhsT=ones_codes[:].bitcast(FP8X4),
                    lhsT_scale=ones_scales[:],
                    rhs=ones_codes[:].bitcast(FP8X4),
                    rhs_scale=ones_scales[:],
                    start=True,
                    stop=True,
                )

        ident_bf16 = sbuf("ident_bf16", [P, P], BF16)
        ident = sbuf("ident", [P, P], F32)
        make_identity(nc, ident_bf16[:])
        nc.scalar.activation(out=ident[:], in_=ident_bf16[:], func=ACT.Identity)
        green_plane = sbuf("green_plane", [P, V], U8)
        embed_plane = sbuf("embed_plane", [P, GROUPS, D], U8)
        nc.vector.memset(green_plane[:].bitcast(I32), 0)
        nc.vector.memset(embed_plane[:].bitcast(I32), 0)
        bias_raw = sbuf("bias_raw", [P, GROUPS, 4], BF16)

        def load_green_scales():
            for q in range(4):
                nc.sync.dma_start(
                    out=green_plane[32 * q : 32 * q + 4, :].bitcast(I32),
                    in_=green_scales[0][4 * q : 4 * q + 4, :].bitcast(I32),
                )

        load_positions(0, 0)
        load_head(0, 0)
        load_positions(0, 1)
        load_head(0, 1)
        load_positions(0, HASH)
        load_green(0)
        load_green_scales()
        load_positions(1, 0)
        nc.sync.dma_start(out=bias_raw[:], in_=bias.rearrange("(g p t) -> p g t", g=GROUPS, t=4))
        load_positions(1, 1)
        load_positions(1, HASH)
        load_head(1, 0)
        load_head(1, 1)
        load_head(2, 0)
        load_green(2)
        load_head(2, 1)
        load_head(3, 0)
        load_head(3, 1)
        embed_codes = []
        for g in range(GROUPS):
            words = sbuf("embed%d" % g, [P, 2 * D], U8)
            nc.sync.dma_start(out=words[:].bitcast(I32), in_=embed_words[g].bitcast(I32))
            embed_codes.append(words)
        for q in range(4):
            nc.sync.dma_start(
                out=embed_plane[32 * q : 32 * q + 4, :, :].bitcast(I32),
                in_=embed_scales[:, 4 * q : 4 * q + 4, :].rearrange("g r n -> r g n").bitcast(I32),
            )


        def turn_pass(h, c, first_bank):
            for b in range(2):
                turn(h, c, b, first_bank + b)
                drain_turned(h, c, b)

        def logit_passes(h, g, c):
            for t in range(4):
                logit_pass(h, g, t, c, 4 + t)

        def prepare_group(g):
            widen_head(g, 0)
            sort_green_codes(g)
            quantize_head(g, 0)
            widen_head(g, 1)
            sort_green_scales(g)
            quantize_head(g, 1)

        def logit_tile(h, g, t, i):
            for c in range(3):
                logit_pass(h, g, t, c, i)
            rectify(h, g, t)

        warm(14)
        turn_pass(0, 0, 0)
        warm(8)
        widen_head(0, 0)
        quantize_pos(0, 0)
        quantize_head(0, 0)
        turn_pass(0, 1, 2)
        widen_head(0, 1)
        quantize_pos(0, 1)
        quantize_head(0, 1)
        for t in range(4):
            logit_pass(0, 0, t, 0, 4 + t)
        turn_pass(0, HASH, 0)
        sort_green_codes(0)
        sort_green_scales(0)
        quantize_pos(0, HASH)
        sort_green_codes(1)
        sort_green_scales(1)
        for t in range(4):
            logit_pass(0, 0, t, 1, 4 + t)
        turn_pass(1, 0, 2)
        sort_words(1, 1, True)
        for t in range(4):
            logit_pass(0, 0, t, HASH, 4 + t)
        rectify(0, 0, 0)
        rectify(0, 0, 1)
        sort_words(1, HASH, True)
        quantize_pos(1, 0)
        turn_pass(1, 1, 0)
        turn_pass(1, HASH, 2)
        rectify(0, 0, 2)
        rectify(0, 0, 3)
        widen_head(1, 0)
        quantize_pos(1, 1)
        quantize_head(1, 0)
        quantize_pos(1, HASH)
        widen_head(1, 1)
        ring = [4, 5, 0, 1, 2, 3, 6, 7]
        for c in range(3):
            for t in range(4):
                logit_pass(1, 0, t, c, ring[t])
        for t in range(4):
            rectify(1, 0, t)
        widen_head(2, 0)
        quantize_head(1, 1)
        sort_green_codes(2)
        quantize_head(2, 0)
        widen_head(2, 1)
        sort_green_scales(2)
        quantize_head(2, 1)
        prepare_group(3)
        for c in (0, HASH, 1):
            for t in range(4):
                logit_pass(0, 1, t, c, ring[4 + t], last=1)
        for t in range(4):
            rectify(0, 1, t)
        steps = [(1, 1), (0, 2), (1, 2), (0, 3), (1, 3)]
        for n, (h, g) in enumerate(steps):
            for t in range(4):
                logit_tile(h, g, t, ring[(4 * n + t) % 8])
        order = [(0, 0), (0, 1), (0, 2), (1, 0), (0, 3), (1, 1), (1, 2), (1, 3)]
        widen_r(*order[0])
        for n in range(1, len(order)):
            widen_r(*order[n])
            quantize_r(*order[n - 1])
        quantize_r(*order[-1])

        blocks = [(h, tile, 512 * d, 512) for h in range(2) for tile in range(4) for d in range(2)]
        blocks = blocks[:-1] + [(1, 3, 512 + P * j, P) for j in range(4)]
        accs = [bank(ring[4 + n]) for n in range(4)]
        for g in range(GROUPS):
            for acc, (h, tile, first, width) in zip(accs, blocks):
                mix_pass(acc, h, tile, g, first, width)
        for acc, block in zip(accs, blocks):
            store(acc, *block, on_vector=False)
        for n in range(4, len(blocks)):
            h, tile, first, width = blocks[n]
            acc = bank(ring[(4 + n) % BANKS])
            for g in range(GROUPS):
                mix_pass(acc, h, tile, g, first, width)
            store(acc, h, tile, first, width, on_vector=(n >= 8 and n % 2 == 1))
